import numpy as np
import ml_dtypes


def mxq(x, axis, fmt="e4m3"):
    dtype, down = {"e4m3": (ml_dtypes.float8_e4m3fn, 7), "e5m2": (ml_dtypes.float8_e5m2, 14)}[fmt]
    v = np.moveaxis(np.asarray(x, np.float32).astype(ml_dtypes.bfloat16).astype(np.float64), axis, -1)
    blocks = v.reshape(v.shape[:-1] + (-1, 32))
    amax = np.abs(blocks).max(-1, keepdims=True)
    byte = np.maximum(np.where(amax > 0, np.frexp(amax)[1] - 1 + 127, 0) - down, 1)
    scale = np.exp2(byte - 127.0)
    codes = (blocks / scale).astype(np.float32).astype(dtype).astype(np.float64)
    return np.moveaxis((codes * scale).reshape(v.shape), -1, axis)


WIDE = False


def mx_kscale(k, group=512):
    if not WIDE:
        return np.ones(k)
    levels = np.array([10, -10, 5, -5, 0])
    if group != 512:
        return np.exp2(np.random.permutation(np.resize(levels, k // group))).repeat(group)
    if k % 512:
        return np.exp2(np.random.permutation(np.resize(levels, k // 32))).repeat(32)
    a = np.empty((k // 512, 16))
    for p in range(k // 512):
        a[p, :8] = np.random.permutation(np.resize(levels, 8))
        for g in range(8):
            far = levels[np.abs(levels - a[p, g]) >= 10]
            a[p, g + 8] = far[np.random.randint(len(far))]
    return np.exp2(a.ravel()).repeat(32)


def f64(x):
    return np.asarray(x).astype(np.float64)


def striped(idx):
    return np.tile(np.asarray(idx).reshape(-1, 16).T, (8, 1)).astype(np.uint16)


def unstriped(offs):
    return offs[:16].T.reshape(-1).astype(np.int64)


H, KV, D, NQ, N = 2, 2, 256, 512, 1024


def setup_inputs():
    n = np.random.standard_normal
    s = mx_kscale(D, 0)[:, None]
    u = mx_kscale(N)
    t = np.random.uniform(0.5, 2.0, N) * u
    v = n((KV, N, 128))
    return {
        "qT": (n((H, D, NQ)) * s * (0.70 / np.sqrt(D))).astype(np.float32),
        "kT": (n((KV, D, N)) / s).astype(np.float32),
        "t": t.reshape(N, 1).astype(np.float32),
        "v": (v / t[:, None]).astype(np.float32),
        "kb": (0.5 * n((N, 1))).astype(np.float32),
        "mask": (np.arange(N)[:, None] <= np.sort(np.random.randint(N // 4, N, NQ))[None, :]).astype(np.float32),
        "og": n((H, NQ, 128)).astype(np.float32),
    }


def reference(qT, kT, t, v, kb, mask, og):
    a = mxq(f64(kT), 1, "e4m3").transpose(0, 2, 1) @ mxq(f64(qT), 1, "e4m3")
    a = a + f64(kb)
    p = a / (1.0 + np.exp(-a))
    p = p * f64(mask)
    w = p * f64(t)
    y = mxq(w, 1, "e4m3").transpose(0, 2, 1) @ mxq(f64(v), 1, "e4m3")
    y = y / 16.0
    y = y / (1.0 + np.exp(-f64(og)))
    return y

from contextlib import ExitStack

import concourse.mybir as mybir

H, D, NQ, N, E = 2, 256, 512, 1024, 128
FLOPS = 2 * H * N * NQ * (D + E)

F32 = mybir.dt.float32
BF16 = mybir.dt.bfloat16
U32 = mybir.dt.uint32
U8 = mybir.dt.uint8
FP8X4 = mybir.dt.float8_e4m3fn_x4
ACT = mybir.ActivationFunctionType
ALU = mybir.AluOpType

P = 128
PACK = 4
ROWS = D // PACK
PASS = P * PACK
PASSES = N // PASS
HALF = NQ // 2
TILE = 128
RUN = 4


def tile_rows_a_silu_kb_mask_gate_kernel(tc, qT, kT, t, v, kb, mask, og, out):
    nc = tc.nc
    with ExitStack() as ctx:
        sb = ctx.enter_context(tc.tile_pool(name="sb", bufs=1))
        ps = ctx.enter_context(tc.psum_pool(name="ps", bufs=1))
        ctx.enter_context(tc.manual_schedule())

        def tile(name, shape, dtype):
            return sb.tile(shape, dtype, name=name, align_bytes=64)

        def quantised(name, values):
            words = values.shape[1] // PACK
            codes = tile(name + "_codes", [P, words], U32)
            scales = tile(name + "_scales", [P, words], U8)
            nc.vector.quantize_mx(out=codes[:].bitcast(FP8X4), scales=scales[:], in_=values)
            return codes, scales

        q_rows = qT.rearrange("h (p j) q -> (h p) j q", j=PACK)
        k_rows = kT.rearrange("h (p j) i -> (h p) j i", j=PACK)
        mask_rows = mask.rearrange("(g p r) q -> g p r q", p=P, r=PACK)

        t_raw = tile("t_raw", [P, PASSES, 8], F32)
        kb_sb = tile("kb_sb", [P, PASSES, 8], F32)
        nc.scalar.dma_start(out=kb_sb[:, :, 0:PACK], in_=kb.rearrange("(g p r) o -> p g (r o)", p=P, r=PACK))
        nc.scalar.dma_start(out=t_raw[:, :, 0:PACK], in_=t.rearrange("(g p r) o -> p g (r o)", p=P, r=PACK))

        def load(name, src):
            dst = tile(name, list(src.shape), F32)
            nc.sync.dma_start(out=dst[:], in_=src)
            return dst

        q_raw, k_raw, mask_raw = {}, {}, {}
        q_raw[0] = load("q_raw0", q_rows[:, :, 0:HALF])
        k_raw[0, 0] = load("k_raw00", k_rows[:, :, 0:256])
        k_raw[0, 1] = load("k_raw01", k_rows[:, :, 256:512])
        mask_raw[0, 0] = load("mask_raw00", mask_rows[0][:, :, 0:HALF])
        q_raw[1] = load("q_raw1", q_rows[:, :, HALF:NQ])
        mask_raw[0, 1] = load("mask_raw01", mask_rows[0][:, :, HALF:NQ])
        k_raw1 = load("k_raw1", k_rows[:, :, 512:1024])
        mask1 = load("mask_raw1", mask_rows[1])
        v_raw = load("v_raw", v.rearrange("h (g p j) e -> p (h g) (j e)", p=P, j=PACK))
        og_raw = load("og_raw", og.rearrange("h (c p) e -> p (h c) e", p=P))

        t_sb = tile("t_sb", [P, PASSES, PACK], F32)
        nc.gpsimd.tensor_scalar(out=t_sb[:], in0=t_raw[:, :, 0:PACK], scalar1=1.0 / 32.0, scalar2=0.0,
                                op0=ALU.mult, op1=ALU.add)

        score_banks = [[ps.tile([P, 512], F32, name="score_%d_%d" % (h, b)) for b in range(2)] for h in range(H)]
        y_banks = [ps.tile([P, 512], F32, name="y_%d" % b) for b in range(4)]

        q_bf, q_mx, k_bf, k_mx, mt, p_sb, w_bf, w_mx, v_bf, v_mx, gate = {}, {}, {}, {}, {}, {}, {}, {}, {}, {}, {}

        def cast_q(a):
            q_bf[a] = tile("q_bf%d" % a, [P, HALF * PACK], BF16)
            nc.vector.tensor_copy(out=q_bf[a][:].rearrange("p (c i j) -> p c j i", i=RUN, j=PACK),
                                  in_=q_raw[a][:].rearrange("p j (c i) -> p c j i", i=RUN))

        def quant_q(a):
            q_mx[a] = quantised("q%d" % a, q_bf[a][:])

        def cast_k(g, src, s0, s1):
            if g not in k_bf:
                k_bf[g] = tile("k_bf%d" % g, [P, PASS * PACK], BF16)
            nc.vector.tensor_copy(out=k_bf[g][:].rearrange("p (r s j) -> p s j r", r=PACK, j=PACK)[:, s0:s1],
                                  in_=src[:].rearrange("p j (s r) -> p s j r", r=PACK))

        def quant_k(g, b):
            k_mx[g, b] = quantised("k%d_%d" % (g, b), k_bf[g][:, 1024 * b:1024 * (b + 1)])

        def mask_src(g, a, r):
            return mask_raw[g, a][:, r, :] if g == 0 else mask1[:, r, HALF * a:HALF * (a + 1)]

        def make_mt(g, a, on_vector):
            mt[g, a] = tile("mt%d_%d" % (g, a), [P, PACK, HALF], F32)
            for r in range(PACK):
                if on_vector:
                    nc.vector.tensor_scalar(out=mt[g, a][:, r, :], in0=mask_src(g, a, r), scalar1=t_sb[:, g, r:r + 1],
                                            scalar2=None, op0=ALU.mult)
                else:
                    nc.scalar.activation(out=mt[g, a][:, r, :], in_=mask_src(g, a, r), func=ACT.Copy,
                                         scale=t_sb[:, g, r:r + 1])

        def scores(g, a, h):
            rows = slice(ROWS * h, ROWS * (h + 1))
            qc, qs = q_mx[a]
            for b in range(2):
                kc, ks = k_mx[g, b]
                for x in range(2):
                    for c in range(2):
                        at = HALF * x + TILE * c
                        nc.tensor.matmul_mx(out=score_banks[h][b][:, at:at + TILE],
                                            lhsT=kc[rows, TILE * x:TILE * (x + 1)].bitcast(FP8X4),
                                            lhsT_scale=ks[rows, TILE * x:TILE * (x + 1)],
                                            rhs=qc[rows, TILE * c:TILE * (c + 1)].bitcast(FP8X4),
                                            rhs_scale=qs[rows, TILE * c:TILE * (c + 1)],
                                            start=True, stop=True)

        def silu(g, a, h):
            p_sb[g, a, h] = tile("p%d_%d_%d" % (g, a, h), [P, PACK, HALF], F32)
            for r in range(PACK):
                b, x = divmod(r, 2)
                nc.scalar.activation(out=p_sb[g, a, h][:, r, :], in_=score_banks[h][b][:, HALF * x:HALF * (x + 1)],
                                     func=ACT.Silu, bias=kb_sb[:, g, r:r + 1])

        def weigh(g, a, h, q0=0, q1=HALF):
            w_bf[g, a, h, q0] = tile("w%d_%d_%d_%d" % (g, a, h, q0), [P, (q1 - q0) * PACK], BF16)
            nc.vector.tensor_tensor(out=w_bf[g, a, h, q0][:].rearrange("p (c i r) -> p c r i", i=RUN, r=PACK),
                                    in0=p_sb[g, a, h][:, :, q0:q1].rearrange("p r (c i) -> p c r i", i=RUN),
                                    in1=mt[g, a][:, :, q0:q1].rearrange("p r (c i) -> p c r i", i=RUN), op=ALU.mult)

        def quant_w(g, a, h, q0=0):
            src = w_bf[g, a, h, q0]
            codes, scales = quantised("w%d_%d_%d_%d" % (g, a, h, q0), src[:])
            for c in range(src.shape[1] // PACK // TILE):
                w_mx[g, a, h, q0 // TILE + c] = (codes[:, TILE * c:TILE * (c + 1)], scales[:, TILE * c:TILE * (c + 1)])

        def cast_v(h, engine_copy):
            v_bf[h] = tile("v_bf%d" % h, [P, PASSES * E * PACK], BF16)
            engine_copy(out=v_bf[h][:].rearrange("p (g c i j) -> p g c j i", g=PASSES, i=RUN, j=PACK),
                        in_=v_raw[:, PASSES * h:PASSES * (h + 1), :].rearrange("p g (j c i) -> p g c j i", j=PACK, i=RUN))

        def quant_v(h):
            v_mx[h] = quantised("v%d" % h, v_bf[h][:])

        def make_gate(a):
            gate[a] = tile("gate%d" % a, [P, H, 2, E], F32)
            nc.scalar.activation(out=gate[a][:], in_=og_raw[:].rearrange("p (h c) e -> p h c e", h=H)[:, :, 2 * a:2 * a + 2, :],
                                 func=ACT.Tanh, scale=0.5)

        def product(a, h, bank, tiles):
            vc, vs = v_mx[h]
            for c in tiles:
                for g in range(PASSES):
                    wc, ws = w_mx[g, a, h, c]
                    nc.tensor.matmul_mx(out=y_banks[bank][:, E * c:E * (c + 1)], lhsT=wc.bitcast(FP8X4), lhsT_scale=ws,
                                        rhs=vc[:, E * g:E * (g + 1)].bitcast(FP8X4), rhs_scale=vs[:, E * g:E * (g + 1)],
                                        start=(g == 0), stop=(g == PASSES - 1))

        def finish(a, h, bank, c0, c1):
            res = tile("res%d_%d_%d" % (a, h, c0), [P, (c1 - c0) * E], F32)
            nc.vector.scalar_tensor_tensor(out=res[:], in0=gate[a][:, h, c0:c1, :].rearrange("p c e -> p (c e)"), scalar=1.0,
                                           in1=y_banks[bank][:, E * c0:E * c1], op0=ALU.add, op1=ALU.mult)
            q0 = HALF * a
            nc.sync.dma_start(out=out[h, q0 + TILE * c0:q0 + TILE * c1, :].rearrange("(c p) e -> p c e", p=P),
                              in_=res[:].rearrange("p (c e) -> p c e", e=E))

        cast_q(0)
        quant_q(0)
        cast_k(0, k_raw[0, 0], 0, 64)
        cast_k(0, k_raw[0, 1], 64, 128)
        quant_k(0, 0)
        quant_k(0, 1)
        scores(0, 0, 0)
        scores(0, 0, 1)
        silu(0, 0, 0)
        silu(0, 0, 1)
        make_mt(0, 0, True)
        cast_q(1)
        weigh(0, 0, 0)
        quant_q(1)
        scores(0, 1, 0)
        scores(0, 1, 1)
        make_mt(0, 1, False)
        silu(0, 1, 0)
        silu(0, 1, 1)
        weigh(0, 0, 1)
        quant_w(0, 0, 0)
        cast_k(1, k_raw1, 0, 128)
        quant_w(0, 0, 1)
        quant_k(1, 0)
        quant_k(1, 1)
        scores(1, 0, 0)
        scores(1, 0, 1)
        make_mt(1, 0, False)
        silu(1, 0, 0)
        silu(1, 0, 1)
        weigh(0, 1, 0)
        weigh(0, 1, 1)
        quant_w(0, 1, 0)
        quant_w(0, 1, 1)
        scores(1, 1, 0)
        scores(1, 1, 1)
        make_mt(1, 1, False)
        cast_v(1, nc.scalar.copy)
        silu(1, 1, 0)
        make_gate(0)
        silu(1, 1, 1)
        make_gate(1)
        weigh(1, 0, 0)
        cast_v(0, nc.vector.tensor_copy)
        quant_w(1, 0, 0)
        quant_v(0)
        weigh(1, 0, 1)
        product(0, 0, 0, (0, 1))
        quant_v(1)
        quant_w(1, 0, 1)
        product(0, 1, 1, (0, 1))
        weigh(1, 1, 0)
        finish(0, 0, 0, 0, 2)
        quant_w(1, 1, 0)
        product(1, 0, 2, (0, 1))
        weigh(1, 1, 1, 0, TILE)
        finish(0, 1, 1, 0, 2)
        quant_w(1, 1, 1, 0)
        product(1, 1, 3, (0,))
        weigh(1, 1, 1, TILE, HALF)
        finish(1, 0, 2, 0, 2)
        quant_w(1, 1, 1, TILE)
        product(1, 1, 0, (1,))
        finish(1, 1, 3, 0, 1)
        finish(1, 1, 0, 1, 2)
